import numpy as np
import ml_dtypes


def mxq(x, axis, fmt="e4m3"):
    dtype, down = {"e4m3": (ml_dtypes.float8_e4m3fn, 7), "e5m2": (ml_dtypes.float8_e5m2, 14)}[fmt]
    v = np.moveaxis(np.asarray(x, np.float32).astype(ml_dtypes.bfloat16).astype(np.float64), axis, -1)
    blocks = v.reshape(v.shape[:-1] + (-1, 32))
    amax = np.abs(blocks).max(-1, keepdims=True)
    byte = np.maximum(np.where(amax > 0, np.frexp(amax)[1] - 1 + 127, 0) - down, 1)
    scale = np.exp2(byte - 127.0)
    codes = (blocks / scale).astype(np.float32).astype(dtype).astype(np.float64)
    return np.moveaxis((codes * scale).reshape(v.shape), -1, axis)


WIDE = False


def mx_kscale(k):
    if not WIDE:
        return np.ones(k)
    levels = np.array([10, -10, 5, -5, 0])
    if k % 512:
        return np.exp2(np.random.permutation(np.resize(levels, k // 32))).repeat(32)
    a = np.empty((k // 512, 16))
    for p in range(k // 512):
        a[p, :8] = np.random.permutation(np.resize(levels, 8))
        for g in range(8):
            far = levels[np.abs(levels - a[p, g]) >= 10]
            a[p, g + 8] = far[np.random.randint(len(far))]
    return np.exp2(a.ravel()).repeat(32)


def f64(x):
    return np.asarray(x).astype(np.float64)


def striped(idx):
    return np.tile(idx.reshape(-1, 16).T, (8, 1)).astype(np.uint16)


def unstriped(offs):
    return offs[:16].T.reshape(-1).astype(np.int64)


E2M1 = np.array([0.0, 0.5, 1.0, 1.5, 2.0, 3.0, 4.0, 6.0, -0.0, -0.5, -1.0, -1.5, -2.0, -3.0, -4.0, -6.0])


def pack_weight(w, fmt):
    k, n = w.shape
    w = f64(np.asarray(w, np.float32).astype(ml_dtypes.bfloat16)).reshape(k // 32, 32, n)
    amax = np.abs(w).max(1)
    if fmt == "e4m3":
        byte = np.frexp(amax)[1] - 1 + 127 - 7
    else:
        mant, ex = np.frexp(amax / 6.0)
        byte = np.where(mant > 0.5, ex, ex - 1) + 127
    byte = np.clip(np.where(amax > 0, byte, 1), 1, 254)
    scaled = (w * np.exp2(127.0 - byte)[:, None, :]).reshape(k, n).astype(np.float32)
    by_word = np.ascontiguousarray(scaled.reshape(k // 512, 128, 4, n).transpose(0, 1, 3, 2))
    if fmt == "e4m3":
        words = by_word.astype(ml_dtypes.float8_e4m3fn).view(np.uint8)
    else:
        c = by_word.astype(ml_dtypes.float4_e2m1fn).view(np.uint8) & 0xF
        words = (c[..., 0::2] | (c[..., 1::2] << 4)).reshape(k // 512, 128, 2 * n)
    return np.ascontiguousarray(words), np.ascontiguousarray(byte.astype(np.uint8).reshape(k // 512, 16, n))


def unpack_weight(words, scales, fmt):
    g, _, n = scales.shape
    words = np.ascontiguousarray(words).reshape(g, 128, n, -1)
    if fmt == "e4m3":
        vals = words.view(ml_dtypes.float8_e4m3fn).astype(np.float64)
    else:
        nib = np.empty((g, 128, n, 4), np.uint8)
        nib[..., 0::2] = words & 0xF
        nib[..., 1::2] = words >> 4
        vals = E2M1[nib]
    vals = vals * np.repeat(np.exp2(scales.astype(np.float64) - 127.0), 8, axis=1)[..., None]
    return vals.transpose(0, 1, 3, 2).reshape(g * 512, n)


def gelu(v):
    return 0.5 * v * (1.0 + np.tanh(np.sqrt(2.0 / np.pi) * (v + 0.044715 * v**3)))


K, T, S, H, N, K2, TN, P = 1024, 4096, 1024, 512, 384, 512, 2048, 512

def setup_inputs():
    n = np.random.standard_normal
    s, s2, u = mx_kscale(K)[:, None], mx_kscale(K2)[:, None], mx_kscale(H)[:, None]
    tab_words, tab_scales = pack_weight(n((K, T)) * s, "e4m3")
    tab2_words, tab2_scales = pack_weight(n((K2, TN)) * s2, "e4m3")
    w4_words, w4_scales = pack_weight(1.2 * n((H, N)) / np.sqrt(H) / u, "e2m1")
    wc_words, wc_scales = pack_weight(1.2 * n((K, N)) / np.sqrt(K) / s, "e4m3")
    return {
        "tab_words": tab_words, "tab_scales": tab_scales,
        "tab2_words": tab2_words, "tab2_scales": tab2_scales,
        "offs": striped(np.random.permutation(T)[:S]),
        "offs2": striped(np.random.permutation(TN)[:P]),
        "pos1": striped(np.random.permutation(S)[:P]),
        "wa": (n((K, H)) / np.sqrt(K) / s * u.T).astype(np.float32),
        "wb": (n((K, H)) / np.sqrt(K) / s * u.T).astype(np.float32),
        "w4_words": w4_words, "w4_scales": w4_scales,
        "wc_words": wc_words, "wc_scales": wc_scales,
        "wd": (0.7 * n((K2, N)) / np.sqrt(K2) / s2).astype(np.float32),
        "res": (0.7 * n((N, P))).astype(np.float32),
    }

def reference(tab_words, tab_scales, tab2_words, tab2_scales, offs, offs2, pos1, wa, wb,
              w4_words, w4_scales, wc_words, wc_scales, wd, res):
    v = unpack_weight(tab_words, tab_scales, "e4m3")[:, unstriped(offs)]
    v2 = unpack_weight(tab2_words, tab2_scales, "e4m3")[:, unstriped(offs2)]
    w4 = unpack_weight(w4_words, w4_scales, "e2m1")
    wc = unpack_weight(wc_words, wc_scales, "e4m3")
    ha = mxq(f64(wa), 0, "e4m3").T @ v
    hb = mxq(f64(wb), 0, "e4m3").T @ v
    h = mxq(np.maximum(ha, hb), 0, "e4m3")
    y = np.tanh(w4.T @ h + wc.T @ v)
    b = mxq(f64(wd), 0, "e4m3").T @ v2
    return y[:, unstriped(pos1)] + np.exp(b) + f64(res)

@@ -1,0 +1,249 @@
+from contextlib import ExitStack
+
+import concourse.mybir as mybir
+
+K, T, S, H, N, K2, TN, PICKS = 1024, 4096, 1024, 512, 384, 512, 2048, 512
+FLOPS = 2 * (2 * K * H * S + H * N * S + K * N * S + K2 * N * PICKS)
+
+F32 = mybir.dt.float32
+BF16 = mybir.dt.bfloat16
+I32 = mybir.dt.int32
+U32 = mybir.dt.uint32
+U16 = mybir.dt.uint16
+U8 = mybir.dt.uint8
+FP8X4 = mybir.dt.float8_e4m3fn_x4
+FP4X4 = mybir.dt.float4_e2m1fn_x4
+ALU = mybir.AluOpType
+ACT = mybir.ActivationFunctionType
+
+P = 128
+PACK = 4
+K_PASS = P * PACK
+PASSES = K // K_PASS
+N_TILES = N // P
+CHUNK = 128
+CHUNKS = S // CHUNK
+BANK = 512
+HALF = P // 2
+GATHER = 256
+
+
+def tile_list_weaning_board_features_kernel(
+    tc, tab_words, tab_scales, tab2_words, tab2_scales, offs, offs2, pos1, wa, wb,
+    w4_words, w4_scales, wc_words, wc_scales, wd, res, out,
+):
+    nc = tc.nc
+    with ExitStack() as ctx:
+        lists = ctx.enter_context(tc.tile_pool(name="lists", bufs=1))
+        sb = ctx.enter_context(tc.tile_pool(name="sb", bufs=1))
+        psum = ctx.enter_context(tc.psum_pool(name="psum", bufs=1))
+
+        def tile(name, shape, dtype):
+            return sb.tile(shape, dtype, name=name, align_bytes=64)
+
+        def bank(b, shape):
+            return psum.tile(shape, F32, name="bank%d" % b, tag="bank%d" % b)
+
+        def load_words(name, src, width):
+            dst = tile(name, [P, width], U32)
+            nc.sync.dma_start(out=dst[:].bitcast(I32), in_=src.rearrange("p c i -> p (c i)").bitcast(I32))
+            return dst
+
+        def load_planes(name, src, first, queue):
+            passes, width = src.shape[0], src.shape[2]
+            dst = tile(name, [P, width], U8)
+            nc.vector.memset(dst[:].bitcast(I32), 0)
+            for q in range(4):
+                row = 32 * q + first
+                queue.dma_start(
+                    out=dst[row : row + 4 * passes, :].bitcast(I32),
+                    in_=src[:, 4 * q : 4 * q + 4, :].bitcast(I32),
+                )
+            return dst
+
+        def load_rows(name, src):
+            dst = tile(name, [P, PACK, src.shape[1]], F32)
+            nc.sync.dma_start(out=dst[:], in_=src.rearrange("(p j) c -> p j c", j=PACK))
+            return dst
+
+        def load_list(name, src):
+            dst = lists.tile([P, src.shape[1]], U16, name=name)
+            nc.sync.dma_start(dst[:], src)
+            return dst
+
+        def copy_on(engine, dst, src):
+            if engine == "scalar":
+                nc.scalar.copy(dst, src)
+            else:
+                nc.vector.tensor_copy(dst, src)
+
+        def deal(name, raw, engine):
+            ms = raw.shape[2] // PACK
+            dst = tile(name, [P, PACK, ms, PACK], BF16)
+            copy_on(engine, dst[:].rearrange("p t m j -> p m j t"), raw.rearrange("p j (m t) -> p m j t", t=PACK))
+            return dst
+
+        def quantize(codes, scales, src):
+            nc.vector.quantize_mx(out=codes.bitcast(FP8X4), scales=scales, in_=src)
+
+        def quantize_half(codes, scales, dealt, half):
+            for t in range(PACK):
+                cols = slice(t * P + half * HALF, t * P + (half + 1) * HALF)
+                quantize(codes[:, cols], scales[:, cols], dealt[:, t, :, :].rearrange("p m j -> p (m j)"))
+
+        def mm(acc, w, ws, x, xs, start, stop):
+            nc.tensor.matmul_mx(out=acc, lhsT=w, lhsT_scale=ws, rhs=x, rhs_scale=xs, start=start, stop=stop)
+
+        wa_raw0 = load_rows("wa_raw0", wa[0:K_PASS, :])
+        tab_s = load_planes("tab_s", tab_scales, 0, nc.sync)
+        wc_s = load_planes("wc_s", wc_scales, 0, nc.gpsimd)
+        w4_s = load_planes("w4_s", w4_scales, 0, nc.gpsimd)
+        tab2_s = load_planes("tab2_s", tab2_scales, 8, nc.gpsimd)
+        idx = load_list("idx", offs)
+        tab_w0 = load_words("tab_w0", tab_words[0], T)
+        wa_raw1 = load_rows("wa_raw1", wa[K_PASS:K, :])
+        tab_w1 = load_words("tab_w1", tab_words[1], T)
+        wb_raw0 = load_rows("wb_raw0", wb[0:K_PASS, :])
+        wb_raw1 = [load_rows("wb_raw1_%d" % hf, wb[K_PASS:K, hf * 256 : (hf + 1) * 256]) for hf in range(2)]
+        wc_all = tile("wc_all", [P, PASSES, N], U32)
+        nc.sync.dma_start(out=wc_all[:].bitcast(I32), in_=wc_words.rearrange("a p c i -> p a (c i)").bitcast(I32))
+        wc_w = [wc_all[:, a, :] for a in range(PASSES)]
+        w4_w = tile("w4_w", [P, 2 * N], U8)
+        nc.sync.dma_start(out=w4_w[:].bitcast(I32), in_=w4_words[0].bitcast(I32))
+        wd_raw = load_rows("wd_raw", wd)
+        idx2 = load_list("idx2", offs2)
+        tab2_w = load_words("tab2_w", tab2_words[0], TN)
+        pick = load_list("pick", pos1)
+        res_sb = tile("res_sb", [P, N_TILES, PICKS], F32)
+        nc.sync.dma_start(out=res_sb[:], in_=res.rearrange("(u p) j -> p u j", p=P))
+
+        wa_raw = [wa_raw0, wa_raw1]
+        tab_w = [tab_w0, tab_w1]
+        wa_c = [tile("wa_c%d" % a, [P, H], U32) for a in range(PASSES)]
+        wa_s = [tile("wa_s%d" % a, [P, H], U8) for a in range(PASSES)]
+        wb_c = [tile("wb_c%d" % a, [P, H], U32) for a in range(PASSES)]
+        wb_s = [tile("wb_s%d" % a, [P, H], U8) for a in range(PASSES)]
+        v_w = [tile("v_w%d" % a, [P, S], U32) for a in range(PASSES)]
+        v_s = tile("v_s", [P, S], U8)
+
+        def h_pass(acc, codes, scales, a, c):
+            cols = slice(c * CHUNK, (c + 1) * CHUNK)
+            for t in range(PACK):
+                wcols = slice(t * P, (t + 1) * P)
+                mm(acc[:, t, :], codes[a][:, wcols].bitcast(FP8X4), scales[a][:, wcols],
+                   v_w[a][:, cols].bitcast(FP8X4), v_s[4 * a : P, cols],
+                   a == 0 and t == 0, a == PASSES - 1 and t == PACK - 1)
+
+        nc.vector.tensor_copy(v_s[:], tab_s[:].indirect(idx[:]))
+        ha_ps = [bank(c, [P, PACK, CHUNK]) for c in range(CHUNKS)]
+        ha_sb = [tile("ha_sb%d" % c, [P, CHUNK, PACK], F32) for c in range(CHUNKS)]
+        for a in range(PASSES):
+            dealt = deal("wa_d%d" % a, wa_raw[a][:], "scalar")
+            quantize(wa_c[a][:], wa_s[a][:], dealt[:].rearrange("p t m j -> p (t m j)"))
+            for g in range(S // GATHER):
+                nc.vector.tensor_copy(
+                    v_w[a][:, g * GATHER : (g + 1) * GATHER],
+                    tab_w[a][:].indirect(idx[:, g * GATHER // 16 : (g + 1) * GATHER // 16]),
+                )
+                for c in range(g * GATHER // CHUNK, (g + 1) * GATHER // CHUNK):
+                    h_pass(ha_ps[c], wa_c, wa_s, a, c)
+
+        def drain_ha(c):
+            nc.scalar.copy(ha_sb[c][:], ha_ps[c][:].rearrange("p t j -> p j t"))
+
+        for c in range(2):
+            drain_ha(c)
+        wb_d00 = deal("wb_d00", wb_raw0[:, :, 0:256], "vector")
+        wb_d01 = deal("wb_d01", wb_raw0[:, :, 256:512], "scalar")
+        for c in range(2, CHUNKS):
+            drain_ha(c)
+        quantize_half(wb_c[0], wb_s[0], wb_d00, 0)
+        wb_d10 = deal("wb_d10", wb_raw1[0][:], "vector")
+        quantize_half(wb_c[0], wb_s[0], wb_d01, 1)
+        quantize_half(wb_c[1], wb_s[1], wb_d10, 0)
+        wb_d11 = deal("wb_d11", wb_raw1[1][:], "vector")
+        quantize_half(wb_c[1], wb_s[1], wb_d11, 1)
+
+        hb_ps = [bank(c, [P, PACK, CHUNK]) for c in range(CHUNKS)]
+        for a in range(PASSES):
+            for c in range(CHUNKS):
+                h_pass(hb_ps[c], wb_c, wb_s, a, c)
+
+        wd_d = tile("wd_d", [P, N, PACK], BF16)
+        nc.scalar.copy(
+            wd_d[:].rearrange("p (c i) j -> p c j i", i=PACK),
+            wd_raw[:].rearrange("p j (c i) -> p c j i", i=PACK),
+        )
+        wd_c = tile("wd_c", [P, N], U32)
+        wd_s = tile("wd_s", [P, N], U8)
+        v2_w = tile("v2_w", [P, PICKS], U32)
+        v2_s = tile("v2_s", [P, PICKS], U8)
+
+        h_c = tile("h_c", [P, S], U32)
+        h_s = tile("h_s", [P, S], U8)
+        h_bf = [tile("h_bf%d" % q, [P, 2, CHUNK * PACK], BF16) for q in range(CHUNKS // 2)]
+        y = [tile("y%d" % u, [P, S], F32) for u in range(N_TILES)]
+
+        def take_max(c):
+            nc.vector.tensor_tensor(
+                h_bf[c // 2][:, c % 2, :].rearrange("p (j t) -> p j t", t=PACK),
+                hb_ps[c][:].rearrange("p t j -> p j t"), ha_sb[c][:], ALU.max,
+            )
+
+        def quantize_h(q):
+            cols = slice(q * 2 * CHUNK, (q + 1) * 2 * CHUNK)
+            quantize(h_c[:, cols], h_s[:, cols], h_bf[q][:].rearrange("p c x -> p (c x)"))
+
+        def y_wc(acc, u, half):
+            cols = slice(half * BANK, (half + 1) * BANK)
+            ncols = slice(u * P, (u + 1) * P)
+            for a in range(PASSES):
+                mm(acc[:], wc_w[a][:, ncols].bitcast(FP8X4), wc_s[4 * a : P, ncols],
+                   v_w[a][:, cols].bitcast(FP8X4), v_s[4 * a : P, cols], a == 0, False)
+
+        def y_w4(acc, u, half):
+            cols = slice(half * BANK, (half + 1) * BANK)
+            mm(acc[:], w4_w[:, 2 * u * P : 2 * (u + 1) * P].bitcast(FP4X4), w4_s[:, u * P : (u + 1) * P],
+               h_c[:, cols].bitcast(FP8X4), h_s[:, cols], False, True)
+            nc.scalar.activation(out=y[u][:, cols], in_=acc[:], func=ACT.Tanh)
+
+        take_max(0)
+        take_max(1)
+        take_max(2)
+        quantize_h(0)
+        take_max(3)
+        take_max(4)
+        quantize_h(1)
+        y0 = [bank(u, [P, BANK]) for u in range(N_TILES)]
+        for u in range(N_TILES):
+            y_wc(y0[u], u, 0)
+        for u in range(N_TILES):
+            y_w4(y0[u], u, 0)
+        quantize(wd_c[:], wd_s[:], wd_d[:].rearrange("p c j -> p (c j)"))
+        nc.vector.tensor_copy(v2_s[:], tab2_s[:].indirect(idx2[:]))
+        nc.vector.tensor_copy(v2_w[:], tab2_w[:].indirect(idx2[:]))
+        take_max(5)
+        take_max(6)
+        quantize_h(2)
+        take_max(7)
+        y1 = [bank(N_TILES + u, [P, BANK]) for u in range(N_TILES)]
+        for u in range(N_TILES):
+            y_wc(y1[u], u, 1)
+        grown = []
+        for u in range(N_TILES):
+            acc = bank(u, [P, BANK])
+            ncols = slice(u * P, (u + 1) * P)
+            mm(acc[:], wd_c[:, ncols].bitcast(FP8X4), wd_s[:, ncols], v2_w[:].bitcast(FP8X4), v2_s[8:P, :], True, True)
+            e = tile("e%d" % u, [P, PICKS], F32)
+            nc.scalar.activation(out=e[:], in_=acc[:], func=ACT.Exp)
+            grown.append(e)
+        quantize_h(3)
+        for u in range(N_TILES):
+            y_w4(y1[u], u, 1)
+        base = [tile("base%d" % u, [P, PICKS], F32) for u in range(N_TILES)]
+        for u in range(N_TILES):
+            nc.vector.tensor_tensor(base[u][:], grown[u][:], res_sb[:, u, :], ALU.add)
+        for u in range(N_TILES):
+            o = tile("o%d" % u, [P, PICKS], F32)
+            nc.vector.tensor_tensor(o[:], y[u][:].indirect(pick[:]), base[u][:], ALU.add)
+            nc.sync.dma_start(out=out[u * P : (u + 1) * P, :], in_=o[:])

@@ -39,7 +39,7 @@ def tile_list_weaning_board_features_kernel(
         psum = ctx.enter_context(tc.psum_pool(name="psum", bufs=1))
 
         def tile(name, shape, dtype):
-            return sb.tile(shape, dtype, name=name, align_bytes=64)
+            return sb.tile(shape, dtype, name=name, tag=name, align_bytes=64)
 
         def bank(b, shape):
             return psum.tile(shape, F32, name="bank%d" % b, tag="bank%d" % b)
@@ -80,7 +80,7 @@ def tile_list_weaning_board_features_kernel(
         def deal(name, raw, engine):
             ms = raw.shape[2] // PACK
             dst = tile(name, [P, PACK, ms, PACK], BF16)
-            copy_on(engine, dst[:].rearrange("p t m j -> p m j t"), raw.rearrange("p j (m t) -> p m j t", t=PACK))
+            copy_on(engine, dst[:].rearrange("p t m j -> p m t j"), raw.rearrange("p j (m t) -> p m t j", t=PACK))
             return dst
 
         def quantize(codes, scales, src):
@@ -95,12 +95,13 @@ def tile_list_weaning_board_features_kernel(
             nc.tensor.matmul_mx(out=acc, lhsT=w, lhsT_scale=ws, rhs=x, rhs_scale=xs, start=start, stop=stop)
 
         wa_raw0 = load_rows("wa_raw0", wa[0:K_PASS, :])
-        tab_s = load_planes("tab_s", tab_scales, 0, nc.sync)
+        tab_s = load_planes("tab_s", tab_scales, 0, nc.gpsimd)
+        tab2_s = load_planes("tab2_s", tab2_scales, 8, nc.gpsimd)
         wc_s = load_planes("wc_s", wc_scales, 0, nc.gpsimd)
         w4_s = load_planes("w4_s", w4_scales, 0, nc.gpsimd)
-        tab2_s = load_planes("tab2_s", tab2_scales, 8, nc.gpsimd)
         idx = load_list("idx", offs)
         tab_w0 = load_words("tab_w0", tab_words[0], T)
+        idx2 = load_list("idx2", offs2)
         wa_raw1 = load_rows("wa_raw1", wa[K_PASS:K, :])
         tab_w1 = load_words("tab_w1", tab_words[1], T)
         wb_raw0 = load_rows("wb_raw0", wb[0:K_PASS, :])
@@ -111,7 +112,6 @@ def tile_list_weaning_board_features_kernel(
         w4_w = tile("w4_w", [P, 2 * N], U8)
         nc.sync.dma_start(out=w4_w[:].bitcast(I32), in_=w4_words[0].bitcast(I32))
         wd_raw = load_rows("wd_raw", wd)
-        idx2 = load_list("idx2", offs2)
         tab2_w = load_words("tab2_w", tab2_words[0], TN)
         pick = load_list("pick", pos1)
         res_sb = tile("res_sb", [P, N_TILES, PICKS], F32)
@@ -135,6 +135,8 @@ def tile_list_weaning_board_features_kernel(
                    a == 0 and t == 0, a == PASSES - 1 and t == PACK - 1)
 
         nc.vector.tensor_copy(v_s[:], tab_s[:].indirect(idx[:]))
+        v2_s = tile("v2_s", [P, PICKS], U8)
+        nc.vector.tensor_copy(v2_s[:], tab2_s[:].indirect(idx2[:]))
         ha_ps = [bank(c, [P, PACK, CHUNK]) for c in range(CHUNKS)]
         ha_sb = [tile("ha_sb%d" % c, [P, CHUNK, PACK], F32) for c in range(CHUNKS)]
         for a in range(PASSES):
@@ -177,11 +179,10 @@ def tile_list_weaning_board_features_kernel(
         wd_c = tile("wd_c", [P, N], U32)
         wd_s = tile("wd_s", [P, N], U8)
         v2_w = tile("v2_w", [P, PICKS], U32)
-        v2_s = tile("v2_s", [P, PICKS], U8)
 
         h_c = tile("h_c", [P, S], U32)
         h_s = tile("h_s", [P, S], U8)
-        h_bf = [tile("h_bf%d" % q, [P, 2, CHUNK * PACK], BF16) for q in range(CHUNKS // 2)]
+        h_bf = [tile("h_bf%d" % q, [P, 2, CHUNK * PACK], BF16) for q in range(CHUNKS // 2 - 1)]
         y = [tile("y%d" % u, [P, S], F32) for u in range(N_TILES)]
 
         def take_max(c):
@@ -219,10 +220,10 @@ def tile_list_weaning_board_features_kernel(
             y_wc(y0[u], u, 0)
         for u in range(N_TILES):
             y_w4(y0[u], u, 0)
-        quantize(wd_c[:], wd_s[:], wd_d[:].rearrange("p c j -> p (c j)"))
-        nc.vector.tensor_copy(v2_s[:], tab2_s[:].indirect(idx2[:]))
-        nc.vector.tensor_copy(v2_w[:], tab2_w[:].indirect(idx2[:]))
         take_max(5)
+        quantize(wd_c[:], wd_s[:], wd_d[:].rearrange("p c j -> p (c j)"))
+        nc.vector.tensor_copy(v2_w[:], tab2_w[:].indirect(idx2[:]))
+        h_bf.append(sb.tile([P, 2, CHUNK * PACK], BF16, name="h_bf_last", tag="tab2_w", align_bytes=64))
         take_max(6)
         quantize_h(2)
         take_max(7)
@@ -244,6 +245,12 @@ def tile_list_weaning_board_features_kernel(
         for u in range(N_TILES):
             nc.vector.tensor_tensor(base[u][:], grown[u][:], res_sb[:, u, :], ALU.add)
         for u in range(N_TILES):
-            o = tile("o%d" % u, [P, PICKS], F32)
-            nc.vector.tensor_tensor(o[:], y[u][:].indirect(pick[:]), base[u][:], ALU.add)
-            nc.sync.dma_start(out=out[u * P : (u + 1) * P, :], in_=o[:])
+            parts = 2 if u == N_TILES - 1 else 1
+            width = PICKS // parts
+            for s in range(parts):
+                cols = slice(s * width, (s + 1) * width)
+                o = tile("o%d_%d" % (u, s), [P, width], F32)
+                nc.vector.tensor_tensor(
+                    o[:], y[u][:].indirect(pick[:, s * width // 16 : (s + 1) * width // 16]), base[u][:, cols], ALU.add
+                )
+                nc.sync.dma_start(out=out[u * P : (u + 1) * P, cols], in_=o[:])

@@ -20,12 +20,13 @@ P = 128
 PACK = 4
 K_PASS = P * PACK
 PASSES = K // K_PASS
+QUADRANTS = 4
 N_TILES = N // P
-CHUNK = 128
-CHUNKS = S // CHUNK
 BANK = 512
-HALF = P // 2
-GATHER = 256
+CHUNK = BANK // PACK
+CHUNKS = S // CHUNK
+LIST_ROWS = 16
+GATHER = 2 * CHUNK
 
 
 def tile_list_weaning_board_features_kernel(
@@ -41,29 +42,41 @@ def tile_list_weaning_board_features_kernel(
         def tile(name, shape, dtype):
             return sb.tile(shape, dtype, name=name, tag=name, align_bytes=64)
 
-        def bank(b, shape):
-            return psum.tile(shape, F32, name="bank%d" % b, tag="bank%d" % b)
+        def bank(number, shape):
+            return psum.tile(shape, F32, name="bank%d" % number, tag="bank%d" % number)
+
+        def zeroed_scales(name, width):
+            dst = tile(name, [P, width], U8)
+            nc.vector.memset(dst[:].bitcast(I32), 0)
+            return dst
 
         def load_words(name, src, width):
             dst = tile(name, [P, width], U32)
             nc.sync.dma_start(out=dst[:].bitcast(I32), in_=src.rearrange("p c i -> p (c i)").bitcast(I32))
             return dst
 
-        def load_planes(name, src, first, queue):
-            passes, width = src.shape[0], src.shape[2]
-            dst = tile(name, [P, width], U8)
-            nc.vector.memset(dst[:].bitcast(I32), 0)
-            for q in range(4):
-                row = 32 * q + first
-                queue.dma_start(
-                    out=dst[row : row + 4 * passes, :].bitcast(I32),
-                    in_=src[:, 4 * q : 4 * q + 4, :].bitcast(I32),
+        def load_wc_scales(dst, quadrants):
+            for q in quadrants:
+                nc.sync.dma_start(
+                    out=dst[32 * q : 32 * q + 8, :].bitcast(I32),
+                    in_=wc_scales[:, 4 * q : 4 * q + 4, :].bitcast(I32),
                 )
-            return dst
+
+        def load_w4_scales(dst):
+            for r in range(4):
+                nc.sync.dma_start(out=dst[r:P:32, :].bitcast(I32), in_=w4_scales[0, r:16:4, :].bitcast(I32))
+
+        def place_scales(dst, spread, first, step):
+            for q in range(QUADRANTS):
+                row = first + 4 * q * step
+                nc.sync.dma_start(
+                    out=dst[32 * q : 32 * q + 4, :].bitcast(I32),
+                    in_=spread[row : row + 4 * step : step, :].bitcast(I32),
+                )
 
         def load_rows(name, src):
             dst = tile(name, [P, PACK, src.shape[1]], F32)
-            nc.sync.dma_start(out=dst[:], in_=src.rearrange("(p j) c -> p j c", j=PACK))
+            nc.sync.dma_start(out=dst[:], in_=src.rearrange("(p i) c -> p i c", i=PACK))
             return dst
 
         def load_list(name, src):
@@ -71,110 +84,106 @@ def tile_list_weaning_board_features_kernel(
             nc.sync.dma_start(dst[:], src)
             return dst
 
-        def copy_on(engine, dst, src):
-            if engine == "scalar":
-                nc.scalar.copy(dst, src)
-            else:
-                nc.vector.tensor_copy(dst, src)
-
-        def deal(name, raw, engine):
-            ms = raw.shape[2] // PACK
-            dst = tile(name, [P, PACK, ms, PACK], BF16)
-            copy_on(engine, dst[:].rearrange("p t m j -> p m t j"), raw.rearrange("p j (m t) -> p m t j", t=PACK))
-            return dst
+        def entries(list_tile, first, count):
+            return list_tile[:, first // LIST_ROWS : (first + count) // LIST_ROWS]
 
         def quantize(codes, scales, src):
             nc.vector.quantize_mx(out=codes.bitcast(FP8X4), scales=scales, in_=src)
 
-        def quantize_half(codes, scales, dealt, half):
-            for t in range(PACK):
-                cols = slice(t * P + half * HALF, t * P + (half + 1) * HALF)
-                quantize(codes[:, cols], scales[:, cols], dealt[:, t, :, :].rearrange("p m j -> p (m j)"))
+        def mm(acc, w, w_scales, x, x_scales, start, stop):
+            nc.tensor.matmul_mx(out=acc, lhsT=w, lhsT_scale=w_scales, rhs=x, rhs_scale=x_scales, start=start, stop=stop)
 
-        def mm(acc, w, ws, x, xs, start, stop):
-            nc.tensor.matmul_mx(out=acc, lhsT=w, lhsT_scale=ws, rhs=x, rhs_scale=xs, start=start, stop=stop)
+        tab_s = tile("tab_s", [P, T], U8)
+        nc.vector.memset(tab_s[:, 0 : T // 2].bitcast(I32), 0)
+        nc.gpsimd.memset(tab_s[:, T // 2 : T].bitcast(I32), 0)
+        tab2_s = tile("tab2_s", [P, TN], U8)
+        nc.gpsimd.memset(tab2_s[:].bitcast(I32), 0)
+        v_s = [zeroed_scales("v_s%d" % a, S) for a in range(PASSES)]
+        wc_s = zeroed_scales("wc_s", N)
+        w4_s = zeroed_scales("w4_s", N)
+        v2_s = zeroed_scales("v2_s", PICKS)
+        v_s_spread = tile("v_s_spread", [P, S], U8)
+        v2_s_spread = tile("v2_s_spread", [P, PICKS], U8)
 
         wa_raw0 = load_rows("wa_raw0", wa[0:K_PASS, :])
-        tab_s = load_planes("tab_s", tab_scales, 0, nc.gpsimd)
-        tab2_s = load_planes("tab2_s", tab2_scales, 8, nc.gpsimd)
-        wc_s = load_planes("wc_s", wc_scales, 0, nc.gpsimd)
-        w4_s = load_planes("w4_s", w4_scales, 0, nc.gpsimd)
         idx = load_list("idx", offs)
-        tab_w0 = load_words("tab_w0", tab_words[0], T)
         idx2 = load_list("idx2", offs2)
+        nc.sync.dma_start(out=tab_s[0:P:4, :].bitcast(I32), in_=tab_scales.rearrange("a q t -> (a q) t").bitcast(I32))
+        nc.sync.dma_start(out=tab2_s[0:P:8, :].bitcast(I32), in_=tab2_scales[0].bitcast(I32))
+        tab_w0 = load_words("tab_w0", tab_words[0], T)
         wa_raw1 = load_rows("wa_raw1", wa[K_PASS:K, :])
+        load_wc_scales(wc_s, range(0, 1))
+        nc.vector.tensor_copy(v_s_spread[:], tab_s[:].indirect(idx[:]))
+        nc.vector.tensor_copy(v2_s_spread[:], tab2_s[:].indirect(idx2[:]))
+        place_scales(v_s[0], v_s_spread, 0, 4)
         tab_w1 = load_words("tab_w1", tab_words[1], T)
+        place_scales(v_s[1], v_s_spread, P // 2, 4)
         wb_raw0 = load_rows("wb_raw0", wb[0:K_PASS, :])
-        wb_raw1 = [load_rows("wb_raw1_%d" % hf, wb[K_PASS:K, hf * 256 : (hf + 1) * 256]) for hf in range(2)]
-        wc_all = tile("wc_all", [P, PASSES, N], U32)
-        nc.sync.dma_start(out=wc_all[:].bitcast(I32), in_=wc_words.rearrange("a p c i -> p a (c i)").bitcast(I32))
-        wc_w = [wc_all[:, a, :] for a in range(PASSES)]
+        load_wc_scales(wc_s, range(1, 2))
+        wb_raw1 = load_rows("wb_raw1", wb[K_PASS:K, :])
+        wd_raw = load_rows("wd_raw", wd)
+        load_wc_scales(wc_s, range(2, QUADRANTS))
+        load_w4_scales(w4_s)
+        wc_w = tile("wc_w", [P, PASSES, N], U32)
+        nc.sync.dma_start(out=wc_w[:].bitcast(I32), in_=wc_words.rearrange("a p c i -> p a (c i)").bitcast(I32))
         w4_w = tile("w4_w", [P, 2 * N], U8)
         nc.sync.dma_start(out=w4_w[:].bitcast(I32), in_=w4_words[0].bitcast(I32))
-        wd_raw = load_rows("wd_raw", wd)
+        place_scales(v2_s, v2_s_spread, 0, 8)
         tab2_w = load_words("tab2_w", tab2_words[0], TN)
-        pick = load_list("pick", pos1)
         res_sb = tile("res_sb", [P, N_TILES, PICKS], F32)
         nc.sync.dma_start(out=res_sb[:], in_=res.rearrange("(u p) j -> p u j", p=P))
+        pick = load_list("pick", pos1)
 
         wa_raw = [wa_raw0, wa_raw1]
+        wb_raw = [wb_raw0, wb_raw1]
         tab_w = [tab_w0, tab_w1]
         wa_c = [tile("wa_c%d" % a, [P, H], U32) for a in range(PASSES)]
         wa_s = [tile("wa_s%d" % a, [P, H], U8) for a in range(PASSES)]
         wb_c = [tile("wb_c%d" % a, [P, H], U32) for a in range(PASSES)]
         wb_s = [tile("wb_s%d" % a, [P, H], U8) for a in range(PASSES)]
         v_w = [tile("v_w%d" % a, [P, S], U32) for a in range(PASSES)]
-        v_s = tile("v_s", [P, S], U8)
 
         def h_pass(acc, codes, scales, a, c):
             cols = slice(c * CHUNK, (c + 1) * CHUNK)
             for t in range(PACK):
-                wcols = slice(t * P, (t + 1) * P)
-                mm(acc[:, t, :], codes[a][:, wcols].bitcast(FP8X4), scales[a][:, wcols],
-                   v_w[a][:, cols].bitcast(FP8X4), v_s[4 * a : P, cols],
+                places = slice(t * P, (t + 1) * P)
+                mm(acc[:, t, :], codes[a][:, places].bitcast(FP8X4), scales[a][:, places],
+                   v_w[a][:, cols].bitcast(FP8X4), v_s[a][:, cols],
                    a == 0 and t == 0, a == PASSES - 1 and t == PACK - 1)
 
-        nc.vector.tensor_copy(v_s[:], tab_s[:].indirect(idx[:]))
-        v2_s = tile("v2_s", [P, PICKS], U8)
-        nc.vector.tensor_copy(v2_s[:], tab2_s[:].indirect(idx2[:]))
         ha_ps = [bank(c, [P, PACK, CHUNK]) for c in range(CHUNKS)]
         ha_sb = [tile("ha_sb%d" % c, [P, CHUNK, PACK], F32) for c in range(CHUNKS)]
         for a in range(PASSES):
-            dealt = deal("wa_d%d" % a, wa_raw[a][:], "scalar")
-            quantize(wa_c[a][:], wa_s[a][:], dealt[:].rearrange("p t m j -> p (t m j)"))
-            for g in range(S // GATHER):
-                nc.vector.tensor_copy(
-                    v_w[a][:, g * GATHER : (g + 1) * GATHER],
-                    tab_w[a][:].indirect(idx[:, g * GATHER // 16 : (g + 1) * GATHER // 16]),
-                )
-                for c in range(g * GATHER // CHUNK, (g + 1) * GATHER // CHUNK):
+            wa_bf = tile("wa_bf%d" % a, [P, PACK, P, PACK], BF16)
+            nc.scalar.copy(
+                wa_bf[:].rearrange("p t m i -> p m t i"), wa_raw[a][:].rearrange("p i (m t) -> p m t i", t=PACK)
+            )
+            quantize(wa_c[a][:], wa_s[a][:], wa_bf[:].rearrange("p t m i -> p (t m i)"))
+            for first in range(0, S, GATHER):
+                nc.vector.tensor_copy(v_w[a][:, first : first + GATHER], tab_w[a][:].indirect(entries(idx, first, GATHER)))
+                for c in range(first // CHUNK, (first + GATHER) // CHUNK):
                     h_pass(ha_ps[c], wa_c, wa_s, a, c)
 
-        def drain_ha(c):
+        for c in range(CHUNKS):
             nc.scalar.copy(ha_sb[c][:], ha_ps[c][:].rearrange("p t j -> p j t"))
 
-        for c in range(2):
-            drain_ha(c)
-        wb_d00 = deal("wb_d00", wb_raw0[:, :, 0:256], "vector")
-        wb_d01 = deal("wb_d01", wb_raw0[:, :, 256:512], "scalar")
-        for c in range(2, CHUNKS):
-            drain_ha(c)
-        quantize_half(wb_c[0], wb_s[0], wb_d00, 0)
-        wb_d10 = deal("wb_d10", wb_raw1[0][:], "vector")
-        quantize_half(wb_c[0], wb_s[0], wb_d01, 1)
-        quantize_half(wb_c[1], wb_s[1], wb_d10, 0)
-        wb_d11 = deal("wb_d11", wb_raw1[1][:], "vector")
-        quantize_half(wb_c[1], wb_s[1], wb_d11, 1)
+        for a in range(PASSES):
+            src = wb_raw[a][:].rearrange("p i (m t) -> p m t i", t=PACK)
+            wb_bf = [tile("wb_bf%d_%d" % (a, e), [P, 2, P, PACK], BF16) for e in range(2)]
+            for e in range(2):
+                nc.vector.tensor_copy(wb_bf[e][:].rearrange("p t m i -> p m t i"), src[:, :, 2 * e : 2 * e + 2, :])
+            for e in range(2):
+                places = slice(e * 2 * P, (e + 1) * 2 * P)
+                quantize(wb_c[a][:, places], wb_s[a][:, places], wb_bf[e][:].rearrange("p t m i -> p (t m i)"))
 
         hb_ps = [bank(c, [P, PACK, CHUNK]) for c in range(CHUNKS)]
         for a in range(PASSES):
             for c in range(CHUNKS):
                 h_pass(hb_ps[c], wb_c, wb_s, a, c)
 
-        wd_d = tile("wd_d", [P, N, PACK], BF16)
+        wd_bf = tile("wd_bf", [P, N, PACK], BF16)
         nc.scalar.copy(
-            wd_d[:].rearrange("p (c i) j -> p c j i", i=PACK),
-            wd_raw[:].rearrange("p j (c i) -> p c j i", i=PACK),
+            wd_bf[:].rearrange("p (c e) i -> p c i e", e=4), wd_raw[:].rearrange("p i (c e) -> p c i e", e=4)
         )
         wd_c = tile("wd_c", [P, N], U32)
         wd_s = tile("wd_s", [P, N], U8)
@@ -182,7 +191,7 @@ def tile_list_weaning_board_features_kernel(
 
         h_c = tile("h_c", [P, S], U32)
         h_s = tile("h_s", [P, S], U8)
-        h_bf = [tile("h_bf%d" % q, [P, 2, CHUNK * PACK], BF16) for q in range(CHUNKS // 2 - 1)]
+        h_bf = [tile("h_bf%d" % pair, [P, 2, CHUNK * PACK], BF16) for pair in range(CHUNKS // 2 - 1)]
         y = [tile("y%d" % u, [P, S], F32) for u in range(N_TILES)]
 
         def take_max(c):
@@ -191,18 +200,18 @@ def tile_list_weaning_board_features_kernel(
                 hb_ps[c][:].rearrange("p t j -> p j t"), ha_sb[c][:], ALU.max,
             )
 
-        def quantize_h(q):
-            cols = slice(q * 2 * CHUNK, (q + 1) * 2 * CHUNK)
-            quantize(h_c[:, cols], h_s[:, cols], h_bf[q][:].rearrange("p c x -> p (c x)"))
+        def quantize_h(pair):
+            cols = slice(pair * 2 * CHUNK, (pair + 1) * 2 * CHUNK)
+            quantize(h_c[:, cols], h_s[:, cols], h_bf[pair][:].rearrange("p c x -> p (c x)"))
 
-        def y_wc(acc, u, half):
+        def y_from_wc(acc, u, half):
             cols = slice(half * BANK, (half + 1) * BANK)
-            ncols = slice(u * P, (u + 1) * P)
+            rows = slice(u * P, (u + 1) * P)
             for a in range(PASSES):
-                mm(acc[:], wc_w[a][:, ncols].bitcast(FP8X4), wc_s[4 * a : P, ncols],
-                   v_w[a][:, cols].bitcast(FP8X4), v_s[4 * a : P, cols], a == 0, False)
+                mm(acc[:], wc_w[:, a, rows].bitcast(FP8X4), wc_s[4 * a : P, rows],
+                   v_w[a][:, cols].bitcast(FP8X4), v_s[a][:, cols], a == 0, False)
 
-        def y_w4(acc, u, half):
+        def y_from_w4(acc, u, half):
             cols = slice(half * BANK, (half + 1) * BANK)
             mm(acc[:], w4_w[:, 2 * u * P : 2 * (u + 1) * P].bitcast(FP4X4), w4_s[:, u * P : (u + 1) * P],
                h_c[:, cols].bitcast(FP8X4), h_s[:, cols], False, True)
@@ -215,42 +224,40 @@ def tile_list_weaning_board_features_kernel(
         take_max(3)
         take_max(4)
         quantize_h(1)
-        y0 = [bank(u, [P, BANK]) for u in range(N_TILES)]
+        y_first = [bank(u, [P, BANK]) for u in range(N_TILES)]
         for u in range(N_TILES):
-            y_wc(y0[u], u, 0)
+            y_from_wc(y_first[u], u, 0)
         for u in range(N_TILES):
-            y_w4(y0[u], u, 0)
+            y_from_w4(y_first[u], u, 0)
         take_max(5)
-        quantize(wd_c[:], wd_s[:], wd_d[:].rearrange("p c j -> p (c j)"))
+        quantize(wd_c[:], wd_s[:], wd_bf[:].rearrange("p c i -> p (c i)"))
         nc.vector.tensor_copy(v2_w[:], tab2_w[:].indirect(idx2[:]))
         h_bf.append(sb.tile([P, 2, CHUNK * PACK], BF16, name="h_bf_last", tag="tab2_w", align_bytes=64))
         take_max(6)
         quantize_h(2)
         take_max(7)
-        y1 = [bank(N_TILES + u, [P, BANK]) for u in range(N_TILES)]
+        y_second = [bank(N_TILES + u, [P, BANK]) for u in range(N_TILES)]
         for u in range(N_TILES):
-            y_wc(y1[u], u, 1)
-        grown = []
+            y_from_wc(y_second[u], u, 1)
+        exp_b = []
         for u in range(N_TILES):
             acc = bank(u, [P, BANK])
-            ncols = slice(u * P, (u + 1) * P)
-            mm(acc[:], wd_c[:, ncols].bitcast(FP8X4), wd_s[:, ncols], v2_w[:].bitcast(FP8X4), v2_s[8:P, :], True, True)
-            e = tile("e%d" % u, [P, PICKS], F32)
-            nc.scalar.activation(out=e[:], in_=acc[:], func=ACT.Exp)
-            grown.append(e)
+            rows = slice(u * P, (u + 1) * P)
+            mm(acc[:], wd_c[:, rows].bitcast(FP8X4), wd_s[:, rows], v2_w[:].bitcast(FP8X4), v2_s[:], True, True)
+            exp_u = tile("exp_b%d" % u, [P, PICKS], F32)
+            nc.scalar.activation(out=exp_u[:], in_=acc[:], func=ACT.Exp)
+            exp_b.append(exp_u)
         quantize_h(3)
         for u in range(N_TILES):
-            y_w4(y1[u], u, 1)
+            y_from_w4(y_second[u], u, 1)
+
         base = [tile("base%d" % u, [P, PICKS], F32) for u in range(N_TILES)]
         for u in range(N_TILES):
-            nc.vector.tensor_tensor(base[u][:], grown[u][:], res_sb[:, u, :], ALU.add)
+            nc.vector.tensor_tensor(base[u][:], exp_b[u][:], res_sb[:, u, :], ALU.add)
         for u in range(N_TILES):
-            parts = 2 if u == N_TILES - 1 else 1
-            width = PICKS // parts
-            for s in range(parts):
-                cols = slice(s * width, (s + 1) * width)
-                o = tile("o%d_%d" % (u, s), [P, width], F32)
-                nc.vector.tensor_tensor(
-                    o[:], y[u][:].indirect(pick[:, s * width // 16 : (s + 1) * width // 16]), base[u][:, cols], ALU.add
-                )
-                nc.sync.dma_start(out=out[u * P : (u + 1) * P, cols], in_=o[:])
+            width = PICKS // 2 if u == N_TILES - 1 else PICKS
+            for first in range(0, PICKS, width):
+                cols = slice(first, first + width)
+                picked = tile("picked%d_%d" % (u, first), [P, width], F32)
+                nc.vector.tensor_tensor(picked[:], y[u][:].indirect(entries(pick, first, width)), base[u][:, cols], ALU.add)
+                nc.sync.dma_start(out=out[u * P : (u + 1) * P, cols], in_=picked[:])

from contextlib import ExitStack

import concourse.mybir as mybir

K, T, S, H, N, K2, TN, PICKS = 1024, 4096, 1024, 512, 384, 512, 2048, 512
FLOPS = 2 * (2 * K * H * S + H * N * S + K * N * S + K2 * N * PICKS)

F32 = mybir.dt.float32
BF16 = mybir.dt.bfloat16
I32 = mybir.dt.int32
U32 = mybir.dt.uint32
U16 = mybir.dt.uint16
U8 = mybir.dt.uint8
FP8X4 = mybir.dt.float8_e4m3fn_x4
FP4X4 = mybir.dt.float4_e2m1fn_x4
ALU = mybir.AluOpType
ACT = mybir.ActivationFunctionType

P = 128
PACK = 4
K_PASS = P * PACK
PASSES = K // K_PASS
QUADRANTS = 4
N_TILES = N // P
BANK = 512
CHUNK = BANK // PACK
CHUNKS = S // CHUNK
LIST_ROWS = 16
GATHER = 2 * CHUNK


def tile_list_weaning_board_features_kernel(
    tc, tab_words, tab_scales, tab2_words, tab2_scales, offs, offs2, pos1, wa, wb,
    w4_words, w4_scales, wc_words, wc_scales, wd, res, out,
):
    nc = tc.nc
    with ExitStack() as ctx:
        lists = ctx.enter_context(tc.tile_pool(name="lists", bufs=1))
        sb = ctx.enter_context(tc.tile_pool(name="sb", bufs=1))
        psum = ctx.enter_context(tc.psum_pool(name="psum", bufs=1))

        def tile(name, shape, dtype):
            return sb.tile(shape, dtype, name=name, tag=name, align_bytes=64)

        def bank(number, shape):
            return psum.tile(shape, F32, name="bank%d" % number, tag="bank%d" % number)

        def zeroed_scales(name, width):
            dst = tile(name, [P, width], U8)
            nc.vector.memset(dst[:].bitcast(I32), 0)
            return dst

        def load_words(name, src, width):
            dst = tile(name, [P, width], U32)
            nc.sync.dma_start(out=dst[:].bitcast(I32), in_=src.rearrange("p c i -> p (c i)").bitcast(I32))
            return dst

        def load_wc_scales(dst, quadrants):
            for q in quadrants:
                nc.sync.dma_start(
                    out=dst[32 * q : 32 * q + 8, :].bitcast(I32),
                    in_=wc_scales[:, 4 * q : 4 * q + 4, :].bitcast(I32),
                )

        def load_w4_scales(dst):
            for r in range(4):
                nc.sync.dma_start(out=dst[r:P:32, :].bitcast(I32), in_=w4_scales[0, r:16:4, :].bitcast(I32))

        def place_scales(dst, spread, first, step):
            for q in range(QUADRANTS):
                row = first + 4 * q * step
                nc.sync.dma_start(
                    out=dst[32 * q : 32 * q + 4, :].bitcast(I32),
                    in_=spread[row : row + 4 * step : step, :].bitcast(I32),
                )

        def load_rows(name, src):
            dst = tile(name, [P, PACK, src.shape[1]], F32)
            nc.sync.dma_start(out=dst[:], in_=src.rearrange("(p i) c -> p i c", i=PACK))
            return dst

        def load_list(name, src):
            dst = lists.tile([P, src.shape[1]], U16, name=name)
            nc.sync.dma_start(dst[:], src)
            return dst

        def entries(list_tile, first, count):
            return list_tile[:, first // LIST_ROWS : (first + count) // LIST_ROWS]

        def quantize(codes, scales, src):
            nc.vector.quantize_mx(out=codes.bitcast(FP8X4), scales=scales, in_=src)

        def mm(acc, w, w_scales, x, x_scales, start, stop):
            nc.tensor.matmul_mx(out=acc, lhsT=w, lhsT_scale=w_scales, rhs=x, rhs_scale=x_scales, start=start, stop=stop)

        tab_s = tile("tab_s", [P, T], U8)
        nc.vector.memset(tab_s[:, 0 : T // 2].bitcast(I32), 0)
        nc.gpsimd.memset(tab_s[:, T // 2 : T].bitcast(I32), 0)
        tab2_s = tile("tab2_s", [P, TN], U8)
        nc.gpsimd.memset(tab2_s[:].bitcast(I32), 0)
        v_s = [zeroed_scales("v_s%d" % a, S) for a in range(PASSES)]
        wc_s = zeroed_scales("wc_s", N)
        w4_s = zeroed_scales("w4_s", N)
        v2_s = zeroed_scales("v2_s", PICKS)
        v_s_spread = tile("v_s_spread", [P, S], U8)
        v2_s_spread = tile("v2_s_spread", [P, PICKS], U8)

        wa_raw0 = load_rows("wa_raw0", wa[0:K_PASS, :])
        idx = load_list("idx", offs)
        idx2 = load_list("idx2", offs2)
        nc.sync.dma_start(out=tab_s[0:P:4, :].bitcast(I32), in_=tab_scales.rearrange("a q t -> (a q) t").bitcast(I32))
        nc.sync.dma_start(out=tab2_s[0:P:8, :].bitcast(I32), in_=tab2_scales[0].bitcast(I32))
        tab_w0 = load_words("tab_w0", tab_words[0], T)
        wa_raw1 = load_rows("wa_raw1", wa[K_PASS:K, :])
        load_wc_scales(wc_s, range(0, 1))
        nc.vector.tensor_copy(v_s_spread[:], tab_s[:].indirect(idx[:]))
        nc.vector.tensor_copy(v2_s_spread[:], tab2_s[:].indirect(idx2[:]))
        place_scales(v_s[0], v_s_spread, 0, 4)
        tab_w1 = load_words("tab_w1", tab_words[1], T)
        place_scales(v_s[1], v_s_spread, P // 2, 4)
        wb_raw0 = load_rows("wb_raw0", wb[0:K_PASS, :])
        load_wc_scales(wc_s, range(1, 2))
        wb_raw1 = load_rows("wb_raw1", wb[K_PASS:K, :])
        wd_raw = load_rows("wd_raw", wd)
        load_wc_scales(wc_s, range(2, QUADRANTS))
        load_w4_scales(w4_s)
        wc_w = tile("wc_w", [P, PASSES, N], U32)
        nc.sync.dma_start(out=wc_w[:].bitcast(I32), in_=wc_words.rearrange("a p c i -> p a (c i)").bitcast(I32))
        w4_w = tile("w4_w", [P, 2 * N], U8)
        nc.sync.dma_start(out=w4_w[:].bitcast(I32), in_=w4_words[0].bitcast(I32))
        place_scales(v2_s, v2_s_spread, 0, 8)
        tab2_w = load_words("tab2_w", tab2_words[0], TN)
        res_sb = tile("res_sb", [P, N_TILES, PICKS], F32)
        nc.sync.dma_start(out=res_sb[:], in_=res.rearrange("(u p) j -> p u j", p=P))
        pick = load_list("pick", pos1)

        wa_raw = [wa_raw0, wa_raw1]
        wb_raw = [wb_raw0, wb_raw1]
        tab_w = [tab_w0, tab_w1]
        wa_c = [tile("wa_c%d" % a, [P, H], U32) for a in range(PASSES)]
        wa_s = [tile("wa_s%d" % a, [P, H], U8) for a in range(PASSES)]
        wb_c = [tile("wb_c%d" % a, [P, H], U32) for a in range(PASSES)]
        wb_s = [tile("wb_s%d" % a, [P, H], U8) for a in range(PASSES)]
        v_w = [tile("v_w%d" % a, [P, S], U32) for a in range(PASSES)]

        def h_pass(acc, codes, scales, a, c):
            cols = slice(c * CHUNK, (c + 1) * CHUNK)
            for t in range(PACK):
                places = slice(t * P, (t + 1) * P)
                mm(acc[:, t, :], codes[a][:, places].bitcast(FP8X4), scales[a][:, places],
                   v_w[a][:, cols].bitcast(FP8X4), v_s[a][:, cols],
                   a == 0 and t == 0, a == PASSES - 1 and t == PACK - 1)

        ha_ps = [bank(c, [P, PACK, CHUNK]) for c in range(CHUNKS)]
        ha_sb = [tile("ha_sb%d" % c, [P, CHUNK, PACK], F32) for c in range(CHUNKS)]
        for a in range(PASSES):
            wa_bf = tile("wa_bf%d" % a, [P, PACK, P, PACK], BF16)
            nc.scalar.copy(
                wa_bf[:].rearrange("p t m i -> p m t i"), wa_raw[a][:].rearrange("p i (m t) -> p m t i", t=PACK)
            )
            quantize(wa_c[a][:], wa_s[a][:], wa_bf[:].rearrange("p t m i -> p (t m i)"))
            for first in range(0, S, GATHER):
                nc.vector.tensor_copy(v_w[a][:, first : first + GATHER], tab_w[a][:].indirect(entries(idx, first, GATHER)))
                for c in range(first // CHUNK, (first + GATHER) // CHUNK):
                    h_pass(ha_ps[c], wa_c, wa_s, a, c)

        for c in range(CHUNKS):
            nc.scalar.copy(ha_sb[c][:], ha_ps[c][:].rearrange("p t j -> p j t"))

        for a in range(PASSES):
            src = wb_raw[a][:].rearrange("p i (m t) -> p m t i", t=PACK)
            wb_bf = [tile("wb_bf%d_%d" % (a, e), [P, 2, P, PACK], BF16) for e in range(2)]
            for e in range(2):
                nc.vector.tensor_copy(wb_bf[e][:].rearrange("p t m i -> p m t i"), src[:, :, 2 * e : 2 * e + 2, :])
            for e in range(2):
                places = slice(e * 2 * P, (e + 1) * 2 * P)
                quantize(wb_c[a][:, places], wb_s[a][:, places], wb_bf[e][:].rearrange("p t m i -> p (t m i)"))

        hb_ps = [bank(c, [P, PACK, CHUNK]) for c in range(CHUNKS)]
        for a in range(PASSES):
            for c in range(CHUNKS):
                h_pass(hb_ps[c], wb_c, wb_s, a, c)

        wd_bf = tile("wd_bf", [P, N, PACK], BF16)
        nc.scalar.copy(
            wd_bf[:].rearrange("p (c e) i -> p c i e", e=4), wd_raw[:].rearrange("p i (c e) -> p c i e", e=4)
        )
        wd_c = tile("wd_c", [P, N], U32)
        wd_s = tile("wd_s", [P, N], U8)
        v2_w = tile("v2_w", [P, PICKS], U32)

        h_c = tile("h_c", [P, S], U32)
        h_s = tile("h_s", [P, S], U8)
        h_bf = [tile("h_bf%d" % pair, [P, 2, CHUNK * PACK], BF16) for pair in range(CHUNKS // 2 - 1)]
        y = [tile("y%d" % u, [P, S], F32) for u in range(N_TILES)]

        def take_max(c):
            nc.vector.tensor_tensor(
                h_bf[c // 2][:, c % 2, :].rearrange("p (j t) -> p j t", t=PACK),
                hb_ps[c][:].rearrange("p t j -> p j t"), ha_sb[c][:], ALU.max,
            )

        def quantize_h(pair):
            cols = slice(pair * 2 * CHUNK, (pair + 1) * 2 * CHUNK)
            quantize(h_c[:, cols], h_s[:, cols], h_bf[pair][:].rearrange("p c x -> p (c x)"))

        def y_from_wc(acc, u, half):
            cols = slice(half * BANK, (half + 1) * BANK)
            rows = slice(u * P, (u + 1) * P)
            for a in range(PASSES):
                mm(acc[:], wc_w[:, a, rows].bitcast(FP8X4), wc_s[4 * a : P, rows],
                   v_w[a][:, cols].bitcast(FP8X4), v_s[a][:, cols], a == 0, False)

        def y_from_w4(acc, u, half):
            cols = slice(half * BANK, (half + 1) * BANK)
            mm(acc[:], w4_w[:, 2 * u * P : 2 * (u + 1) * P].bitcast(FP4X4), w4_s[:, u * P : (u + 1) * P],
               h_c[:, cols].bitcast(FP8X4), h_s[:, cols], False, True)
            nc.scalar.activation(out=y[u][:, cols], in_=acc[:], func=ACT.Tanh)

        take_max(0)
        take_max(1)
        take_max(2)
        quantize_h(0)
        take_max(3)
        take_max(4)
        quantize_h(1)
        y_first = [bank(u, [P, BANK]) for u in range(N_TILES)]
        for u in range(N_TILES):
            y_from_wc(y_first[u], u, 0)
        for u in range(N_TILES):
            y_from_w4(y_first[u], u, 0)
        take_max(5)
        quantize(wd_c[:], wd_s[:], wd_bf[:].rearrange("p c i -> p (c i)"))
        nc.vector.tensor_copy(v2_w[:], tab2_w[:].indirect(idx2[:]))
        h_bf.append(sb.tile([P, 2, CHUNK * PACK], BF16, name="h_bf_last", tag="tab2_w", align_bytes=64))
        take_max(6)
        quantize_h(2)
        take_max(7)
        y_second = [bank(N_TILES + u, [P, BANK]) for u in range(N_TILES)]
        for u in range(N_TILES):
            y_from_wc(y_second[u], u, 1)
        exp_b = []
        for u in range(N_TILES):
            acc = bank(u, [P, BANK])
            rows = slice(u * P, (u + 1) * P)
            mm(acc[:], wd_c[:, rows].bitcast(FP8X4), wd_s[:, rows], v2_w[:].bitcast(FP8X4), v2_s[:], True, True)
            exp_u = tile("exp_b%d" % u, [P, PICKS], F32)
            nc.scalar.activation(out=exp_u[:], in_=acc[:], func=ACT.Exp)
            exp_b.append(exp_u)
        quantize_h(3)
        for u in range(N_TILES):
            y_from_w4(y_second[u], u, 1)

        base = [tile("base%d" % u, [P, PICKS], F32) for u in range(N_TILES)]
        for u in range(N_TILES):
            nc.vector.tensor_tensor(base[u][:], exp_b[u][:], res_sb[:, u, :], ALU.add)
        for u in range(N_TILES):
            width = PICKS // 2 if u == N_TILES - 1 else PICKS
            for first in range(0, PICKS, width):
                cols = slice(first, first + width)
                picked = tile("picked%d_%d" % (u, first), [P, width], F32)
                nc.vector.tensor_tensor(picked[:], y[u][:].indirect(entries(pick, first, width)), base[u][:, cols], ALU.add)
                nc.sync.dma_start(out=out[u * P : (u + 1) * P, cols], in_=picked[:])
